import numpy as np
import ml_dtypes


def mxq(x, axis, fmt="e4m3"):
    dtype, down = {"e4m3": (ml_dtypes.float8_e4m3fn, 7), "e5m2": (ml_dtypes.float8_e5m2, 14)}[fmt]
    v = np.moveaxis(np.asarray(x, np.float32).astype(ml_dtypes.bfloat16).astype(np.float64), axis, -1)
    blocks = v.reshape(v.shape[:-1] + (-1, 32))
    amax = np.abs(blocks).max(-1, keepdims=True)
    byte = np.maximum(np.where(amax > 0, np.frexp(amax)[1] - 1 + 127, 0) - down, 1)
    scale = np.exp2(byte - 127.0)
    codes = (blocks / scale).astype(np.float32).astype(dtype).astype(np.float64)
    return np.moveaxis((codes * scale).reshape(v.shape), -1, axis)


WIDE = False


def mx_kscale(k):
    if not WIDE:
        return np.ones(k)
    levels = np.array([10, -10, 5, -5, 0])
    if k % 512:
        return np.exp2(np.random.permutation(np.resize(levels, k // 32))).repeat(32)
    a = np.empty((k // 512, 16))
    for p in range(k // 512):
        a[p, :8] = np.random.permutation(np.resize(levels, 8))
        for g in range(8):
            far = levels[np.abs(levels - a[p, g]) >= 10]
            a[p, g + 8] = far[np.random.randint(len(far))]
    return np.exp2(a.ravel()).repeat(32)


def f64(x):
    return np.asarray(x).astype(np.float64)


def striped(idx):
    return np.tile(idx.reshape(-1, 16).T, (8, 1)).astype(np.uint16)


def unstriped(offs):
    return offs[:16].T.reshape(-1).astype(np.int64)


def pack_weight(w):
    k, n = w.shape
    w = f64(np.asarray(w, np.float32).astype(ml_dtypes.bfloat16)).reshape(k // 32, 32, n)
    amax = np.abs(w).max(1)
    byte = np.clip(np.where(amax > 0, np.frexp(amax)[1] - 1 + 127 - 7, 1), 1, 254)
    scaled = (w * np.exp2(127.0 - byte)[:, None, :]).reshape(k, n).astype(np.float32)
    words = np.ascontiguousarray(scaled.reshape(k // 512, 128, 4, n).transpose(0, 1, 3, 2)).astype(ml_dtypes.float8_e4m3fn).view(np.uint8)
    return words, np.ascontiguousarray(byte.astype(np.uint8).reshape(k // 512, 16, n))


def unpack_weight(words, scales):
    g, p, n, _ = words.shape
    vals = np.ascontiguousarray(words).view(ml_dtypes.float8_e4m3fn).astype(np.float64) * np.repeat(np.exp2(scales.astype(np.float64) - 127.0), 8, axis=1)[..., None]
    return vals.transpose(0, 1, 3, 2).reshape(g * 512, n)


K, T, S, N, H, U, W = 512, 1024, 512, 256, 512, 1024, 512


def setup_inputs():
    n = np.random.standard_normal
    s = mx_kscale(K)[:, None]
    u = mx_kscale(H)
    near = np.random.permutation(U)
    packed_xT = pack_weight(n((K, T)) * s)
    return {
        "x_words": packed_xT[0],
        "x_scales": packed_xT[1],
        "w1": (n((K, H)) / np.sqrt(K) / s).astype(np.float32),
        "grid": (n((H, U))).astype(np.float32),
        "rob": (np.random.uniform(0.3, 0.9, (H, 1))).astype(np.float32),
        "unit": (np.random.uniform(0.6, 1.4, (H, 1)) * u[:, None]).astype(np.float32),
        "w2": (n((H, N)) / np.sqrt(H) / u[:, None]).astype(np.float32),
        "offs": striped(np.random.permutation(T)[:S]),
        "gh": striped(np.random.permutation(U)[:S]),
        "inn": striped(np.random.permutation(U)[:S]),
        "c0": striped(near[:W]),
        "c1": striped(near[W:]),
        "c2": striped(np.random.permutation(U)[:W]),
    }


def reference(x_words, x_scales, w1, grid, rob, unit, w2, offs, gh, inn, c0, c1, c2):
    xq = unpack_weight(x_words, x_scales)[:, unstriped(offs)]
    y = mxq(f64(w1), 0, "e4m3").T @ xq
    insd = f64(grid)[:, unstriped(inn)]
    robin = 0.8 * np.tanh(y) + f64(rob) * (insd - f64(grid)[:, unstriped(gh)])
    gnew = f64(grid).copy()
    gnew[:, unstriped(gh)] = robin
    g_c1 = gnew[:, unstriped(c1)]
    g_c2 = gnew[:, unstriped(c2)]
    g_c0 = gnew[:, unstriped(c0)]
    lap = g_c1 + g_c2 - (1.6 * g_c0)
    hid = f64(unit) * lap
    return mxq(f64(w2), 0, "e4m3").T @ mxq(hid, 0, "e4m3")

@@ -1,0 +1,205 @@
+from contextlib import ExitStack
+
+import concourse.mybir as mybir
+from concourse.masks import make_identity
+
+K, T, S, N, H, U, W = 512, 1024, 512, 256, 512, 1024, 512
+FLOPS = 2 * K * H * S + 2 * H * N * W
+
+F32 = mybir.dt.float32
+BF16 = mybir.dt.bfloat16
+I32 = mybir.dt.int32
+U32 = mybir.dt.uint32
+U16 = mybir.dt.uint16
+U8 = mybir.dt.uint8
+FP8X4 = mybir.dt.float8_e4m3fn_x4
+ALU = mybir.AluOpType
+ACT = mybir.ActivationFunctionType
+
+P = 128
+PACK = 4
+BLOCKS = W // P
+
+
+def tile_picked_yhalos_lap_p_kernel(
+    tc, x_words, x_scales, w1, grid, rob, unit, w2, offs, gh, inn, c0, c1, c2, out
+):
+    nc = tc.nc
+    with ExitStack() as ctx:
+        keep = ctx.enter_context(tc.tile_pool(name="keep", bufs=1))
+        psum = ctx.enter_context(tc.psum_pool(name="psum", bufs=1))
+
+        def load_list(name, src):
+            tile = keep.tile([P, src.shape[1]], U16, name=name)
+            nc.sync.dma_start(tile[:], src)
+            return tile
+
+        grid_rows = grid.rearrange("(p t) c -> t p c", t=PACK)
+        field = [keep.tile([P, U], F32, name="field%d" % t) for t in range(PACK)]
+        x_w = keep.tile([P, T], U32, name="x_w")
+        x_s = keep.tile([P, T], U8, name="x_s")
+        w1_raw = keep.tile([P, PACK, H], F32, name="w1_raw")
+        w2_raw = keep.tile([P, PACK, N], F32, name="w2_raw")
+        rob_sb = keep.tile([P, PACK], F32, name="rob_sb")
+        unit_sb = keep.tile([P, H], F32, name="unit_sb")
+        ident = keep.tile([P, P], F32, name="ident")
+
+        nc.gpsimd.memset(x_s[:].bitcast(I32), 0)
+        nc.scalar.dma_start(rob_sb[:], rob.rearrange("(p t) o -> p (t o)", t=PACK))
+        make_identity(nc, ident[:])
+
+        nc.sync.dma_start(field[0][:], grid_rows[0])
+        inn_l = load_list("inn_l", inn)
+        gh_l = load_list("gh_l", gh)
+        nc.sync.dma_start(field[1][:], grid_rows[1])
+        nc.sync.dma_start(x_w[:].bitcast(I32), x_words[0].rearrange("p n t -> p (n t)").bitcast(I32))
+        for q in range(4):
+            nc.sync.dma_start(
+                x_s[32 * q : 32 * q + 4, :].bitcast(I32), x_scales[0, 4 * q : 4 * q + 4, :].bitcast(I32)
+            )
+        offs_l = load_list("offs_l", offs)
+        nc.sync.dma_start(w1_raw[:], w1.rearrange("(p j) c -> p j c", j=PACK))
+        nc.sync.dma_start(field[2][:], grid_rows[2])
+        nc.sync.dma_start(field[3][:], grid_rows[3])
+        c1_l = load_list("c1_l", c1)
+        c2_l = load_list("c2_l", c2)
+        c0_l = load_list("c0_l", c0)
+        nc.sync.dma_start(w2_raw[:], w2.rearrange("(p j) c -> p j c", j=PACK))
+        nc.sync.dma_start(unit_sb[:], unit.rearrange("h o -> (h o)").partition_broadcast(P))
+
+        inner = [keep.tile([P, S], F32, name="inner%d" % t) for t in range(PACK)]
+        ghost = [keep.tile([P, S], F32, name="ghost%d" % t) for t in range(PACK)]
+
+        def look_up_grid(t):
+            weighted = keep.tile([P, U], F32, name="weighted%d" % t)
+            nc.vector.tensor_scalar(weighted[:], field[t][:], rob_sb[:, t : t + 1], None, ALU.mult)
+            nc.scalar.activation(ghost[t][:], weighted[:].indirect(gh_l[:]), ACT.Copy)
+            nc.scalar.activation(inner[t][:], weighted[:].indirect(inn_l[:]), ACT.Copy)
+
+        look_up_grid(0)
+        look_up_grid(1)
+
+        xg_w = keep.tile([P, S], U32, name="xg_w", align_bytes=64)
+        xg_s = keep.tile([P, S], U8, name="xg_s", align_bytes=64)
+        nc.vector.tensor_copy(xg_w[:], x_w[:].indirect(offs_l[:]))
+        nc.vector.tensor_copy(xg_s[:], x_s[:].indirect(offs_l[:]))
+
+        w1_bf = keep.tile([P, PACK * H], BF16, name="w1_bf", align_bytes=64)
+        w1_c = keep.tile([P, H], U32, name="w1_c", align_bytes=64)
+        w1_s = keep.tile([P, H], U8, name="w1_s", align_bytes=64)
+        nc.vector.tensor_copy(
+            w1_bf[:].rearrange("p (t m j) -> p m j t", t=PACK, j=PACK),
+            w1_raw[:].rearrange("p j (m t) -> p m j t", t=PACK),
+        )
+        for t in range(PACK):
+            cols = slice(t * P, (t + 1) * P)
+            nc.vector.quantize_mx(
+                out=w1_c[:, cols].bitcast(FP8X4), scales=w1_s[:, cols], in_=w1_bf[:, t * H : (t + 1) * H]
+            )
+
+        lap_t = [psum.tile([P, PACK, P], F32, name="lap_t%d" % b) for b in range(BLOCKS)]
+
+        def stencil_tiles(t):
+            return [keep.tile([P, W], F32, name="g%d_%d" % (term, t)) for term in range(3)]
+
+        def add_up(t, g, blocks):
+            for term in range(3):
+                for b in blocks:
+                    nc.tensor.matmul(
+                        lap_t[b][:, t, :],
+                        lhsT=g[term][:, b * P : (b + 1) * P],
+                        rhs=ident[:],
+                        is_transpose=True,
+                        start=(term == 0),
+                        stop=(term == 2),
+                    )
+
+        g2 = stencil_tiles(2)
+        bounded = [keep.tile([P, S], F32, name="bounded%d" % t) for t in range(PACK)]
+        part = [keep.tile([P, S], F32, name="part%d" % t) for t in range(PACK)]
+        for t in range(PACK):
+            cols = slice(t * P, (t + 1) * P)
+            y = psum.tile([P, S], F32, name="y", tag="work", bufs=2)
+            nc.tensor.matmul_mx(
+                out=y[:],
+                lhsT=w1_c[:, cols].bitcast(FP8X4),
+                lhsT_scale=w1_s[:, cols],
+                rhs=xg_w[:].bitcast(FP8X4),
+                rhs_scale=xg_s[:],
+                start=True,
+                stop=True,
+            )
+            if t >= 2:
+                look_up_grid(t)
+            nc.scalar.activation(bounded[t][:], y[:], ACT.Tanh)
+            nc.vector.scalar_tensor_tensor(part[t][:], bounded[t][:], 0.8, ghost[t][:], ALU.mult, ALU.subtract)
+            nc.vector.tensor_tensor(field[t][:].indirect(gh_l[:]), part[t][:], inner[t][:], ALU.add)
+            if t == 2:
+                nc.vector.tensor_copy(g2[0][:], field[t][:].indirect(c1_l[:]))
+
+        w2_bf = keep.tile([P, N, PACK], BF16, name="w2_bf", align_bytes=64)
+        w2_c = keep.tile([P, N], U32, name="w2_c", align_bytes=64)
+        w2_s = keep.tile([P, N], U8, name="w2_s", align_bytes=64)
+        nc.vector.tensor_copy(
+            w2_bf[:].rearrange("p (c i) j -> p c j i", i=PACK),
+            w2_raw[:].rearrange("p j (c i) -> p c j i", i=PACK),
+        )
+        nc.vector.quantize_mx(
+            out=w2_c[:].bitcast(FP8X4), scales=w2_s[:], in_=w2_bf[:].rearrange("p c j -> p (c j)")
+        )
+
+
+        g0 = stencil_tiles(0)
+        g1 = stencil_tiles(1)
+        for t, g in ((0, g0), (1, g1), (2, g2)):
+            if t < 2:
+                nc.scalar.activation(g[0][:], field[t][:].indirect(c1_l[:]), ACT.Copy)
+            nc.scalar.activation(g[1][:], field[t][:].indirect(c2_l[:]), ACT.Copy)
+            nc.scalar.activation(g[2][:], field[t][:].indirect(c0_l[:]), ACT.Copy, scale=-1.6)
+            add_up(t, g, range(BLOCKS))
+
+        g3 = stencil_tiles(PACK - 1)
+        for half in range(2):
+            cols = slice(half * (W // 2), (half + 1) * (W // 2))
+            ent = slice(half * (W // 32), (half + 1) * (W // 32))
+            last = field[PACK - 1]
+            nc.vector.tensor_copy(g3[0][:, cols], last[:].indirect(c1_l[:, ent]))
+            nc.scalar.activation(g3[1][:, cols], last[:].indirect(c2_l[:, ent]), ACT.Copy)
+            nc.scalar.activation(g3[2][:, cols], last[:].indirect(c0_l[:, ent]), ACT.Copy, scale=-1.6)
+            add_up(PACK - 1, g3, range(2 * half, 2 * half + 2))
+
+        unit_v = unit_sb[:].rearrange("w (p u e) -> w u p e", u=2, e=2)
+        out_v = out.rearrange("(h m) w -> m h w", m=P)
+        for b in range(BLOCKS):
+            hid_t = keep.tile([P, H], BF16, name="hid_t%d" % b)
+            nc.vector.tensor_tensor(
+                hid_t[:].rearrange("w (u p e) -> w u p e", u=2, e=2),
+                lap_t[b][:].rearrange("w (u e) p -> w u p e", e=2),
+                unit_v,
+                ALU.mult,
+            )
+            pairs = psum.tile([P, 2, P], F32, name="pairs", tag="work", bufs=2)
+            for u in range(2):
+                nc.tensor.transpose(pairs[:, u, :], hid_t[:].bitcast(F32)[:, u * P : (u + 1) * P], ident[:])
+            hid = keep.tile([P, PACK * P], BF16, name="hid%d" % b, align_bytes=64)
+            nc.scalar.copy(
+                hid[:].bitcast(F32).rearrange("p (w u) -> p w u", u=2), pairs[:].rearrange("p u w -> p w u")
+            )
+            hid_c = keep.tile([P, P], U32, name="hid_c%d" % b, align_bytes=64)
+            hid_s = keep.tile([P, P], U8, name="hid_s%d" % b, align_bytes=64)
+            nc.vector.quantize_mx(out=hid_c[:].bitcast(FP8X4), scales=hid_s[:], in_=hid[:])
+            acc = psum.tile([P, 2, P], F32, name="acc", tag="acc", bufs=2)
+            for h in range(2):
+                cols = slice(h * P, (h + 1) * P)
+                nc.tensor.matmul_mx(
+                    out=acc[:, h, :],
+                    lhsT=w2_c[:, cols].bitcast(FP8X4),
+                    lhsT_scale=w2_s[:, cols],
+                    rhs=hid_c[:].bitcast(FP8X4),
+                    rhs_scale=hid_s[:],
+                    start=True,
+                    stop=True,
+                )
+            res = keep.tile([P, 2, P], F32, name="res%d" % b)
+            nc.scalar.copy(res[:], acc[:])
+            nc.sync.dma_start(out_v[:, :, b * P : (b + 1) * P], res[:])

@@ -19,6 +19,7 @@ ACT = mybir.ActivationFunctionType
 P = 128
 PACK = 4
 BLOCKS = W // P
+W1_SPLIT = 96
 
 
 def tile_picked_yhalos_lap_p_kernel(
@@ -45,6 +46,10 @@ def tile_picked_yhalos_lap_p_kernel(
         ident = keep.tile([P, P], F32, name="ident")
 
         nc.gpsimd.memset(x_s[:].bitcast(I32), 0)
+        warm_in = keep.tile([P, 1], F32, name="warm_in")
+        warm_out = keep.tile([P, 1], F32, name="warm_out")
+        nc.vector.memset(warm_in[:], 0.0)
+        nc.scalar.activation(warm_out[:], warm_in[:], ACT.Tanh)
         nc.scalar.dma_start(rob_sb[:], rob.rearrange("(p t) o -> p (t o)", t=PACK))
         make_identity(nc, ident[:])
 
@@ -53,11 +58,11 @@ def tile_picked_yhalos_lap_p_kernel(
         gh_l = load_list("gh_l", gh)
         nc.sync.dma_start(field[1][:], grid_rows[1])
         nc.sync.dma_start(x_w[:].bitcast(I32), x_words[0].rearrange("p n t -> p (n t)").bitcast(I32))
+        offs_l = load_list("offs_l", offs)
         for q in range(4):
             nc.sync.dma_start(
                 x_s[32 * q : 32 * q + 4, :].bitcast(I32), x_scales[0, 4 * q : 4 * q + 4, :].bitcast(I32)
             )
-        offs_l = load_list("offs_l", offs)
         nc.sync.dma_start(w1_raw[:], w1.rearrange("(p j) c -> p j c", j=PACK))
         nc.sync.dma_start(field[2][:], grid_rows[2])
         nc.sync.dma_start(field[3][:], grid_rows[3])
@@ -74,7 +79,10 @@ def tile_picked_yhalos_lap_p_kernel(
             weighted = keep.tile([P, U], F32, name="weighted%d" % t)
             nc.vector.tensor_scalar(weighted[:], field[t][:], rob_sb[:, t : t + 1], None, ALU.mult)
             nc.scalar.activation(ghost[t][:], weighted[:].indirect(gh_l[:]), ACT.Copy)
-            nc.scalar.activation(inner[t][:], weighted[:].indirect(inn_l[:]), ACT.Copy)
+            if t == 0:
+                nc.vector.tensor_copy(inner[t][:], weighted[:].indirect(inn_l[:]))
+            else:
+                nc.scalar.activation(inner[t][:], weighted[:].indirect(inn_l[:]), ACT.Copy)
 
         look_up_grid(0)
         look_up_grid(1)
@@ -87,10 +95,10 @@ def tile_picked_yhalos_lap_p_kernel(
         w1_bf = keep.tile([P, PACK * H], BF16, name="w1_bf", align_bytes=64)
         w1_c = keep.tile([P, H], U32, name="w1_c", align_bytes=64)
         w1_s = keep.tile([P, H], U8, name="w1_s", align_bytes=64)
-        nc.vector.tensor_copy(
-            w1_bf[:].rearrange("p (t m j) -> p m j t", t=PACK, j=PACK),
-            w1_raw[:].rearrange("p j (m t) -> p m j t", t=PACK),
-        )
+        w1_dst = w1_bf[:].rearrange("p (t m j) -> p m j t", t=PACK, j=PACK)
+        w1_src = w1_raw[:].rearrange("p j (m t) -> p m j t", t=PACK)
+        nc.vector.tensor_copy(w1_dst[:, :W1_SPLIT], w1_src[:, :W1_SPLIT])
+        nc.scalar.copy(w1_dst[:, W1_SPLIT:], w1_src[:, W1_SPLIT:])
         for t in range(PACK):
             cols = slice(t * P, (t + 1) * P)
             nc.vector.quantize_mx(
@@ -134,8 +142,6 @@ def tile_picked_yhalos_lap_p_kernel(
             nc.scalar.activation(bounded[t][:], y[:], ACT.Tanh)
             nc.vector.scalar_tensor_tensor(part[t][:], bounded[t][:], 0.8, ghost[t][:], ALU.mult, ALU.subtract)
             nc.vector.tensor_tensor(field[t][:].indirect(gh_l[:]), part[t][:], inner[t][:], ALU.add)
-            if t == 2:
-                nc.vector.tensor_copy(g2[0][:], field[t][:].indirect(c1_l[:]))
 
         w2_bf = keep.tile([P, N, PACK], BF16, name="w2_bf", align_bytes=64)
         w2_c = keep.tile([P, N], U32, name="w2_c", align_bytes=64)
@@ -152,7 +158,7 @@ def tile_picked_yhalos_lap_p_kernel(
         g0 = stencil_tiles(0)
         g1 = stencil_tiles(1)
         for t, g in ((0, g0), (1, g1), (2, g2)):
-            if t < 2:
+            if t < 3:
                 nc.scalar.activation(g[0][:], field[t][:].indirect(c1_l[:]), ACT.Copy)
             nc.scalar.activation(g[1][:], field[t][:].indirect(c2_l[:]), ACT.Copy)
             nc.scalar.activation(g[2][:], field[t][:].indirect(c0_l[:]), ACT.Copy, scale=-1.6)
@@ -164,7 +170,10 @@ def tile_picked_yhalos_lap_p_kernel(
             ent = slice(half * (W // 32), (half + 1) * (W // 32))
             last = field[PACK - 1]
             nc.vector.tensor_copy(g3[0][:, cols], last[:].indirect(c1_l[:, ent]))
-            nc.scalar.activation(g3[1][:, cols], last[:].indirect(c2_l[:, ent]), ACT.Copy)
+            if half == 0:
+                nc.vector.tensor_copy(g3[1][:, cols], last[:].indirect(c2_l[:, ent]))
+            else:
+                nc.scalar.activation(g3[1][:, cols], last[:].indirect(c2_l[:, ent]), ACT.Copy)
             nc.scalar.activation(g3[2][:, cols], last[:].indirect(c0_l[:, ent]), ACT.Copy, scale=-1.6)
             add_up(PACK - 1, g3, range(2 * half, 2 * half + 2))
 

@@ -19,7 +19,6 @@ ACT = mybir.ActivationFunctionType
 P = 128
 PACK = 4
 BLOCKS = W // P
-W1_SPLIT = 96
 
 
 def tile_picked_yhalos_lap_p_kernel(
@@ -35,7 +34,7 @@ def tile_picked_yhalos_lap_p_kernel(
             nc.sync.dma_start(tile[:], src)
             return tile
 
-        grid_rows = grid.rearrange("(p t) c -> t p c", t=PACK)
+        grid_rows = grid.rearrange("(t p) c -> t p c", p=P)
         field = [keep.tile([P, U], F32, name="field%d" % t) for t in range(PACK)]
         x_w = keep.tile([P, T], U32, name="x_w")
         x_s = keep.tile([P, T], U8, name="x_s")
@@ -50,7 +49,8 @@ def tile_picked_yhalos_lap_p_kernel(
         warm_out = keep.tile([P, 1], F32, name="warm_out")
         nc.vector.memset(warm_in[:], 0.0)
         nc.scalar.activation(warm_out[:], warm_in[:], ACT.Tanh)
-        nc.scalar.dma_start(rob_sb[:], rob.rearrange("(p t) o -> p (t o)", t=PACK))
+        with nc.allow_non_contiguous_dma(reason="one weight for each partition and plane"):
+            nc.scalar.dma_start(rob_sb[:], rob.rearrange("(t p) o -> p (t o)", p=P))
         make_identity(nc, ident[:])
 
         nc.sync.dma_start(field[0][:], grid_rows[0])
@@ -72,10 +72,11 @@ def tile_picked_yhalos_lap_p_kernel(
         nc.sync.dma_start(w2_raw[:], w2.rearrange("(p j) c -> p j c", j=PACK))
         nc.sync.dma_start(unit_sb[:], unit.rearrange("h o -> (h o)").partition_broadcast(P))
 
-        inner = [keep.tile([P, S], F32, name="inner%d" % t) for t in range(PACK)]
-        ghost = [keep.tile([P, S], F32, name="ghost%d" % t) for t in range(PACK)]
+        inner, ghost = {}, {}
 
         def look_up_grid(t):
+            ghost[t] = keep.tile([P, S], F32, name="ghost%d" % t, tag="looked%d" % (2 * t), align_bytes=64)
+            inner[t] = keep.tile([P, S], F32, name="inner%d" % t, tag="looked%d" % (2 * t + 1), align_bytes=64)
             weighted = keep.tile([P, U], F32, name="weighted%d" % t)
             nc.vector.tensor_scalar(weighted[:], field[t][:], rob_sb[:, t : t + 1], None, ALU.mult)
             nc.scalar.activation(ghost[t][:], weighted[:].indirect(gh_l[:]), ACT.Copy)
@@ -93,16 +94,21 @@ def tile_picked_yhalos_lap_p_kernel(
         nc.vector.tensor_copy(xg_s[:], x_s[:].indirect(offs_l[:]))
 
         w1_bf = keep.tile([P, PACK * H], BF16, name="w1_bf", align_bytes=64)
-        w1_c = keep.tile([P, H], U32, name="w1_c", align_bytes=64)
+        w1_c = [
+            keep.tile([P, P], U32, name="w1_c%d" % t, tag="looked%d" % (t + 4), align_bytes=64) for t in range(PACK)
+        ]
         w1_s = keep.tile([P, H], U8, name="w1_s", align_bytes=64)
-        w1_dst = w1_bf[:].rearrange("p (t m j) -> p m j t", t=PACK, j=PACK)
-        w1_src = w1_raw[:].rearrange("p j (m t) -> p m j t", t=PACK)
-        nc.vector.tensor_copy(w1_dst[:, :W1_SPLIT], w1_src[:, :W1_SPLIT])
-        nc.scalar.copy(w1_dst[:, W1_SPLIT:], w1_src[:, W1_SPLIT:])
+        w1_dst = w1_bf[:].rearrange("p (t c i j) -> p t c j i", t=PACK, i=PACK, j=PACK)
+        w1_src = w1_raw[:].rearrange("p j (t c i) -> p t c j i", t=PACK, i=PACK)
+        for t in range(PACK):
+            if t < PACK - 1:
+                nc.vector.tensor_copy(w1_dst[:, t], w1_src[:, t])
+            else:
+                nc.scalar.copy(w1_dst[:, t], w1_src[:, t])
         for t in range(PACK):
             cols = slice(t * P, (t + 1) * P)
             nc.vector.quantize_mx(
-                out=w1_c[:, cols].bitcast(FP8X4), scales=w1_s[:, cols], in_=w1_bf[:, t * H : (t + 1) * H]
+                out=w1_c[t][:].bitcast(FP8X4), scales=w1_s[:, cols], in_=w1_bf[:, t * H : (t + 1) * H]
             )
 
         lap_t = [psum.tile([P, PACK, P], F32, name="lap_t%d" % b) for b in range(BLOCKS)]
@@ -130,16 +136,17 @@ def tile_picked_yhalos_lap_p_kernel(
             y = psum.tile([P, S], F32, name="y", tag="work", bufs=2)
             nc.tensor.matmul_mx(
                 out=y[:],
-                lhsT=w1_c[:, cols].bitcast(FP8X4),
+                lhsT=w1_c[t][:].bitcast(FP8X4),
                 lhsT_scale=w1_s[:, cols],
                 rhs=xg_w[:].bitcast(FP8X4),
                 rhs_scale=xg_s[:],
                 start=True,
                 stop=True,
             )
-            if t >= 2:
-                look_up_grid(t)
             nc.scalar.activation(bounded[t][:], y[:], ACT.Tanh)
+            if t % 2 == 1:
+                look_up_grid(2 + t // 2)
+        for t in range(PACK):
             nc.vector.scalar_tensor_tensor(part[t][:], bounded[t][:], 0.8, ghost[t][:], ALU.mult, ALU.subtract)
             nc.vector.tensor_tensor(field[t][:].indirect(gh_l[:]), part[t][:], inner[t][:], ALU.add)
 
@@ -177,19 +184,13 @@ def tile_picked_yhalos_lap_p_kernel(
             nc.scalar.activation(g3[2][:, cols], last[:].indirect(c0_l[:, ent]), ACT.Copy, scale=-1.6)
             add_up(PACK - 1, g3, range(2 * half, 2 * half + 2))
 
-        unit_v = unit_sb[:].rearrange("w (p u e) -> w u p e", u=2, e=2)
         out_v = out.rearrange("(h m) w -> m h w", m=P)
         for b in range(BLOCKS):
             hid_t = keep.tile([P, H], BF16, name="hid_t%d" % b)
-            nc.vector.tensor_tensor(
-                hid_t[:].rearrange("w (u p e) -> w u p e", u=2, e=2),
-                lap_t[b][:].rearrange("w (u e) p -> w u p e", e=2),
-                unit_v,
-                ALU.mult,
-            )
+            nc.vector.tensor_tensor(hid_t[:], lap_t[b][:].rearrange("w t p -> w (t p)"), unit_sb[:], ALU.mult)
             pairs = psum.tile([P, 2, P], F32, name="pairs", tag="work", bufs=2)
             for u in range(2):
-                nc.tensor.transpose(pairs[:, u, :], hid_t[:].bitcast(F32)[:, u * P : (u + 1) * P], ident[:])
+                nc.tensor.transpose(pairs[:, u, :], hid_t[:].bitcast(F32)[:, u::2], ident[:])
             hid = keep.tile([P, PACK * P], BF16, name="hid%d" % b, align_bytes=64)
             nc.scalar.copy(
                 hid[:].bitcast(F32).rearrange("p (w u) -> p w u", u=2), pairs[:].rearrange("p u w -> p w u")

@@ -18,7 +18,13 @@ ACT = mybir.ActivationFunctionType
 
 P = 128
 PACK = 4
+QUADRANT = 32
+ENTRIES_PER_COLUMN = 16
+MX_ALIGN = 64
+ROW_TILES = H // P
 BLOCKS = W // P
+TERMS = 3
+W1_TILES_ON_VECTOR = 2
 
 
 def tile_picked_yhalos_lap_p_kernel(
@@ -35,12 +41,12 @@ def tile_picked_yhalos_lap_p_kernel(
             return tile
 
         grid_rows = grid.rearrange("(t p) c -> t p c", p=P)
-        field = [keep.tile([P, U], F32, name="field%d" % t) for t in range(PACK)]
+        field = [keep.tile([P, U], F32, name="field%d" % t) for t in range(ROW_TILES)]
         x_w = keep.tile([P, T], U32, name="x_w")
         x_s = keep.tile([P, T], U8, name="x_s")
         w1_raw = keep.tile([P, PACK, H], F32, name="w1_raw")
         w2_raw = keep.tile([P, PACK, N], F32, name="w2_raw")
-        rob_sb = keep.tile([P, PACK], F32, name="rob_sb")
+        rob_sb = keep.tile([P, ROW_TILES], F32, name="rob_sb")
         unit_sb = keep.tile([P, H], F32, name="unit_sb")
         ident = keep.tile([P, P], F32, name="ident")
 
@@ -49,7 +55,7 @@ def tile_picked_yhalos_lap_p_kernel(
         warm_out = keep.tile([P, 1], F32, name="warm_out")
         nc.vector.memset(warm_in[:], 0.0)
         nc.scalar.activation(warm_out[:], warm_in[:], ACT.Tanh)
-        with nc.allow_non_contiguous_dma(reason="one weight for each partition and plane"):
+        with nc.allow_non_contiguous_dma(reason="one weight for each partition and row tile"):
             nc.scalar.dma_start(rob_sb[:], rob.rearrange("(t p) o -> p (t o)", p=P))
         make_identity(nc, ident[:])
 
@@ -59,9 +65,10 @@ def tile_picked_yhalos_lap_p_kernel(
         nc.sync.dma_start(field[1][:], grid_rows[1])
         nc.sync.dma_start(x_w[:].bitcast(I32), x_words[0].rearrange("p n t -> p (n t)").bitcast(I32))
         offs_l = load_list("offs_l", offs)
-        for q in range(4):
+        for q in range(P // QUADRANT):
             nc.sync.dma_start(
-                x_s[32 * q : 32 * q + 4, :].bitcast(I32), x_scales[0, 4 * q : 4 * q + 4, :].bitcast(I32)
+                x_s[QUADRANT * q : QUADRANT * q + 4, :].bitcast(I32),
+                x_scales[0, 4 * q : 4 * q + 4, :].bitcast(I32),
             )
         nc.sync.dma_start(w1_raw[:], w1.rearrange("(p j) c -> p j c", j=PACK))
         nc.sync.dma_start(field[2][:], grid_rows[2])
@@ -75,8 +82,8 @@ def tile_picked_yhalos_lap_p_kernel(
         inner, ghost = {}, {}
 
         def look_up_grid(t):
-            ghost[t] = keep.tile([P, S], F32, name="ghost%d" % t, tag="looked%d" % (2 * t), align_bytes=64)
-            inner[t] = keep.tile([P, S], F32, name="inner%d" % t, tag="looked%d" % (2 * t + 1), align_bytes=64)
+            ghost[t] = keep.tile([P, S], F32, name="ghost%d" % t, tag="looked%d" % (2 * t), align_bytes=MX_ALIGN)
+            inner[t] = keep.tile([P, S], F32, name="inner%d" % t, tag="looked%d" % (2 * t + 1), align_bytes=MX_ALIGN)
             weighted = keep.tile([P, U], F32, name="weighted%d" % t)
             nc.vector.tensor_scalar(weighted[:], field[t][:], rob_sb[:, t : t + 1], None, ALU.mult)
             nc.scalar.activation(ghost[t][:], weighted[:].indirect(gh_l[:]), ACT.Copy)
@@ -88,56 +95,53 @@ def tile_picked_yhalos_lap_p_kernel(
         look_up_grid(0)
         look_up_grid(1)
 
-        xg_w = keep.tile([P, S], U32, name="xg_w", align_bytes=64)
-        xg_s = keep.tile([P, S], U8, name="xg_s", align_bytes=64)
+        xg_w = keep.tile([P, S], U32, name="xg_w", align_bytes=MX_ALIGN)
+        xg_s = keep.tile([P, S], U8, name="xg_s", align_bytes=MX_ALIGN)
         nc.vector.tensor_copy(xg_w[:], x_w[:].indirect(offs_l[:]))
         nc.vector.tensor_copy(xg_s[:], x_s[:].indirect(offs_l[:]))
 
-        w1_bf = keep.tile([P, PACK * H], BF16, name="w1_bf", align_bytes=64)
+        w1_bf = keep.tile([P, PACK * H], BF16, name="w1_bf", align_bytes=MX_ALIGN)
         w1_c = [
-            keep.tile([P, P], U32, name="w1_c%d" % t, tag="looked%d" % (t + 4), align_bytes=64) for t in range(PACK)
+            keep.tile([P, P], U32, name="w1_c%d" % t, tag="looked%d" % (t + ROW_TILES), align_bytes=MX_ALIGN)
+            for t in range(ROW_TILES)
         ]
-        w1_s = keep.tile([P, H], U8, name="w1_s", align_bytes=64)
-        w1_dst = w1_bf[:].rearrange("p (t c i j) -> p t c j i", t=PACK, i=PACK, j=PACK)
-        w1_src = w1_raw[:].rearrange("p j (t c i) -> p t c j i", t=PACK, i=PACK)
-        for t in range(PACK):
-            if t < PACK - 1:
+        w1_s = keep.tile([P, H], U8, name="w1_s", align_bytes=MX_ALIGN)
+        w1_dst = w1_bf[:].rearrange("p (t c i j) -> p t c j i", t=ROW_TILES, i=4, j=PACK)
+        w1_src = w1_raw[:].rearrange("p j (t c i) -> p t c j i", t=ROW_TILES, i=4)
+        for t in range(ROW_TILES):
+            if t < W1_TILES_ON_VECTOR:
                 nc.vector.tensor_copy(w1_dst[:, t], w1_src[:, t])
             else:
                 nc.scalar.copy(w1_dst[:, t], w1_src[:, t])
-        for t in range(PACK):
-            cols = slice(t * P, (t + 1) * P)
+        for t in range(ROW_TILES):
             nc.vector.quantize_mx(
-                out=w1_c[t][:].bitcast(FP8X4), scales=w1_s[:, cols], in_=w1_bf[:, t * H : (t + 1) * H]
+                out=w1_c[t][:].bitcast(FP8X4),
+                scales=w1_s[:, t * P : (t + 1) * P],
+                in_=w1_bf[:, t * PACK * P : (t + 1) * PACK * P],
             )
 
-        lap_t = [psum.tile([P, PACK, P], F32, name="lap_t%d" % b) for b in range(BLOCKS)]
+        lap_t = [psum.tile([P, ROW_TILES, P], F32, name="lap_t%d" % b, tag="block%d" % b) for b in range(BLOCKS)]
 
-        def stencil_tiles(t):
-            return [keep.tile([P, W], F32, name="g%d_%d" % (term, t)) for term in range(3)]
-
-        def add_up(t, g, blocks):
-            for term in range(3):
+        def add_up(t, terms, blocks):
+            for term in range(TERMS):
                 for b in blocks:
                     nc.tensor.matmul(
                         lap_t[b][:, t, :],
-                        lhsT=g[term][:, b * P : (b + 1) * P],
+                        lhsT=terms[term][:, b * P : (b + 1) * P],
                         rhs=ident[:],
                         is_transpose=True,
                         start=(term == 0),
-                        stop=(term == 2),
+                        stop=(term == TERMS - 1),
                     )
 
-        g2 = stencil_tiles(2)
-        bounded = [keep.tile([P, S], F32, name="bounded%d" % t) for t in range(PACK)]
-        part = [keep.tile([P, S], F32, name="part%d" % t) for t in range(PACK)]
-        for t in range(PACK):
-            cols = slice(t * P, (t + 1) * P)
+        bounded = [keep.tile([P, S], F32, name="bounded%d" % t) for t in range(ROW_TILES)]
+        part = [keep.tile([P, S], F32, name="part%d" % t) for t in range(ROW_TILES)]
+        for t in range(ROW_TILES):
             y = psum.tile([P, S], F32, name="y", tag="work", bufs=2)
             nc.tensor.matmul_mx(
                 out=y[:],
                 lhsT=w1_c[t][:].bitcast(FP8X4),
-                lhsT_scale=w1_s[:, cols],
+                lhsT_scale=w1_s[:, t * P : (t + 1) * P],
                 rhs=xg_w[:].bitcast(FP8X4),
                 rhs_scale=xg_s[:],
                 start=True,
@@ -146,70 +150,71 @@ def tile_picked_yhalos_lap_p_kernel(
             nc.scalar.activation(bounded[t][:], y[:], ACT.Tanh)
             if t % 2 == 1:
                 look_up_grid(2 + t // 2)
-        for t in range(PACK):
+        for t in range(ROW_TILES):
             nc.vector.scalar_tensor_tensor(part[t][:], bounded[t][:], 0.8, ghost[t][:], ALU.mult, ALU.subtract)
             nc.vector.tensor_tensor(field[t][:].indirect(gh_l[:]), part[t][:], inner[t][:], ALU.add)
 
-        w2_bf = keep.tile([P, N, PACK], BF16, name="w2_bf", align_bytes=64)
-        w2_c = keep.tile([P, N], U32, name="w2_c", align_bytes=64)
-        w2_s = keep.tile([P, N], U8, name="w2_s", align_bytes=64)
+        w2_bf = keep.tile([P, N, PACK], BF16, name="w2_bf", align_bytes=MX_ALIGN)
+        w2_c = keep.tile([P, N], U32, name="w2_c", align_bytes=MX_ALIGN)
+        w2_s = keep.tile([P, N], U8, name="w2_s", align_bytes=MX_ALIGN)
         nc.vector.tensor_copy(
-            w2_bf[:].rearrange("p (c i) j -> p c j i", i=PACK),
-            w2_raw[:].rearrange("p j (c i) -> p c j i", i=PACK),
+            w2_bf[:].rearrange("p (c i) j -> p c j i", i=4),
+            w2_raw[:].rearrange("p j (c i) -> p c j i", i=4),
         )
-        nc.vector.quantize_mx(
-            out=w2_c[:].bitcast(FP8X4), scales=w2_s[:], in_=w2_bf[:].rearrange("p c j -> p (c j)")
-        )
+        nc.vector.quantize_mx(out=w2_c[:].bitcast(FP8X4), scales=w2_s[:], in_=w2_bf[:].rearrange("p c j -> p (c j)"))
 
+        terms = [
+            [keep.tile([P, W], F32, name="term%d_%d" % (term, t)) for term in range(TERMS)] for t in range(ROW_TILES)
+        ]
+        last = ROW_TILES - 1
+        for t in range(last):
+            nc.scalar.activation(terms[t][0][:], field[t][:].indirect(c1_l[:]), ACT.Copy)
+            nc.scalar.activation(terms[t][1][:], field[t][:].indirect(c2_l[:]), ACT.Copy)
+            nc.scalar.activation(terms[t][2][:], field[t][:].indirect(c0_l[:]), ACT.Copy, scale=-1.6)
+            add_up(t, terms[t], range(BLOCKS))
 
-        g0 = stencil_tiles(0)
-        g1 = stencil_tiles(1)
-        for t, g in ((0, g0), (1, g1), (2, g2)):
-            if t < 3:
-                nc.scalar.activation(g[0][:], field[t][:].indirect(c1_l[:]), ACT.Copy)
-            nc.scalar.activation(g[1][:], field[t][:].indirect(c2_l[:]), ACT.Copy)
-            nc.scalar.activation(g[2][:], field[t][:].indirect(c0_l[:]), ACT.Copy, scale=-1.6)
-            add_up(t, g, range(BLOCKS))
-
-        g3 = stencil_tiles(PACK - 1)
+        half_w, half_columns, half_blocks = W // 2, W // 2 // ENTRIES_PER_COLUMN, BLOCKS // 2
         for half in range(2):
-            cols = slice(half * (W // 2), (half + 1) * (W // 2))
-            ent = slice(half * (W // 32), (half + 1) * (W // 32))
-            last = field[PACK - 1]
-            nc.vector.tensor_copy(g3[0][:, cols], last[:].indirect(c1_l[:, ent]))
+            stencils = slice(half * half_w, (half + 1) * half_w)
+            entries = slice(half * half_columns, (half + 1) * half_columns)
+            nc.vector.tensor_copy(terms[last][0][:, stencils], field[last][:].indirect(c1_l[:, entries]))
             if half == 0:
-                nc.vector.tensor_copy(g3[1][:, cols], last[:].indirect(c2_l[:, ent]))
+                nc.vector.tensor_copy(terms[last][1][:, stencils], field[last][:].indirect(c2_l[:, entries]))
             else:
-                nc.scalar.activation(g3[1][:, cols], last[:].indirect(c2_l[:, ent]), ACT.Copy)
-            nc.scalar.activation(g3[2][:, cols], last[:].indirect(c0_l[:, ent]), ACT.Copy, scale=-1.6)
-            add_up(PACK - 1, g3, range(2 * half, 2 * half + 2))
+                nc.scalar.activation(terms[last][1][:, stencils], field[last][:].indirect(c2_l[:, entries]), ACT.Copy)
+            nc.scalar.activation(
+                terms[last][2][:, stencils], field[last][:].indirect(c0_l[:, entries]), ACT.Copy, scale=-1.6
+            )
+            add_up(last, terms[last], range(half * half_blocks, (half + 1) * half_blocks))
 
         out_v = out.rearrange("(h m) w -> m h w", m=P)
         for b in range(BLOCKS):
             hid_t = keep.tile([P, H], BF16, name="hid_t%d" % b)
             nc.vector.tensor_tensor(hid_t[:], lap_t[b][:].rearrange("w t p -> w (t p)"), unit_sb[:], ALU.mult)
-            pairs = psum.tile([P, 2, P], F32, name="pairs", tag="work", bufs=2)
+            pairs = psum.tile([P, 2, P], F32, name="pairs", tag="work" if b < 2 else "spare", bufs=2)
             for u in range(2):
                 nc.tensor.transpose(pairs[:, u, :], hid_t[:].bitcast(F32)[:, u::2], ident[:])
-            hid = keep.tile([P, PACK * P], BF16, name="hid%d" % b, align_bytes=64)
+            hid = keep.tile([P, PACK * P], BF16, name="hid%d" % b, align_bytes=MX_ALIGN)
             nc.scalar.copy(
                 hid[:].bitcast(F32).rearrange("p (w u) -> p w u", u=2), pairs[:].rearrange("p u w -> p w u")
             )
-            hid_c = keep.tile([P, P], U32, name="hid_c%d" % b, align_bytes=64)
-            hid_s = keep.tile([P, P], U8, name="hid_s%d" % b, align_bytes=64)
+            hid_c = keep.tile([P, P], U32, name="hid_c%d" % b, align_bytes=MX_ALIGN)
+            hid_s = keep.tile([P, P], U8, name="hid_s%d" % b, align_bytes=MX_ALIGN)
             nc.vector.quantize_mx(out=hid_c[:].bitcast(FP8X4), scales=hid_s[:], in_=hid[:])
-            acc = psum.tile([P, 2, P], F32, name="acc", tag="acc", bufs=2)
-            for h in range(2):
-                cols = slice(h * P, (h + 1) * P)
+            acc = psum.tile([P, N // P, P], F32, name="acc", tag="block%d" % b)
+            for h in range(N // P):
                 nc.tensor.matmul_mx(
                     out=acc[:, h, :],
-                    lhsT=w2_c[:, cols].bitcast(FP8X4),
-                    lhsT_scale=w2_s[:, cols],
+                    lhsT=w2_c[:, h * P : (h + 1) * P].bitcast(FP8X4),
+                    lhsT_scale=w2_s[:, h * P : (h + 1) * P],
                     rhs=hid_c[:].bitcast(FP8X4),
                     rhs_scale=hid_s[:],
                     start=True,
                     stop=True,
                 )
-            res = keep.tile([P, 2, P], F32, name="res%d" % b)
-            nc.scalar.copy(res[:], acc[:])
+            res = keep.tile([P, N // P, P], F32, name="res%d" % b)
+            if b == BLOCKS - 2:
+                nc.vector.tensor_copy(res[:], acc[:])
+            else:
+                nc.scalar.copy(res[:], acc[:])
             nc.sync.dma_start(out_v[:, :, b * P : (b + 1) * P], res[:])

@@ -51,10 +51,6 @@ def tile_picked_yhalos_lap_p_kernel(
         ident = keep.tile([P, P], F32, name="ident")
 
         nc.gpsimd.memset(x_s[:].bitcast(I32), 0)
-        warm_in = keep.tile([P, 1], F32, name="warm_in")
-        warm_out = keep.tile([P, 1], F32, name="warm_out")
-        nc.vector.memset(warm_in[:], 0.0)
-        nc.scalar.activation(warm_out[:], warm_in[:], ACT.Tanh)
         with nc.allow_non_contiguous_dma(reason="one weight for each partition and row tile"):
             nc.scalar.dma_start(rob_sb[:], rob.rearrange("(t p) o -> p (t o)", p=P))
         make_identity(nc, ident[:])

from contextlib import ExitStack

import concourse.mybir as mybir
from concourse.masks import make_identity

K, T, S, N, H, U, W = 512, 1024, 512, 256, 512, 1024, 512
FLOPS = 2 * K * H * S + 2 * H * N * W

F32 = mybir.dt.float32
BF16 = mybir.dt.bfloat16
I32 = mybir.dt.int32
U32 = mybir.dt.uint32
U16 = mybir.dt.uint16
U8 = mybir.dt.uint8
FP8X4 = mybir.dt.float8_e4m3fn_x4
ALU = mybir.AluOpType
ACT = mybir.ActivationFunctionType

P = 128
PACK = 4
QUADRANT = 32
ENTRIES_PER_COLUMN = 16
MX_ALIGN = 64
ROW_TILES = H // P
BLOCKS = W // P
TERMS = 3
W1_TILES_ON_VECTOR = 2


def tile_picked_yhalos_lap_p_kernel(
    tc, x_words, x_scales, w1, grid, rob, unit, w2, offs, gh, inn, c0, c1, c2, out
):
    nc = tc.nc
    with ExitStack() as ctx:
        keep = ctx.enter_context(tc.tile_pool(name="keep", bufs=1))
        psum = ctx.enter_context(tc.psum_pool(name="psum", bufs=1))

        def load_list(name, src):
            tile = keep.tile([P, src.shape[1]], U16, name=name)
            nc.sync.dma_start(tile[:], src)
            return tile

        grid_rows = grid.rearrange("(t p) c -> t p c", p=P)
        field = [keep.tile([P, U], F32, name="field%d" % t) for t in range(ROW_TILES)]
        x_w = keep.tile([P, T], U32, name="x_w")
        x_s = keep.tile([P, T], U8, name="x_s")
        w1_raw = keep.tile([P, PACK, H], F32, name="w1_raw")
        w2_raw = keep.tile([P, PACK, N], F32, name="w2_raw")
        rob_sb = keep.tile([P, ROW_TILES], F32, name="rob_sb")
        unit_sb = keep.tile([P, H], F32, name="unit_sb")
        ident = keep.tile([P, P], F32, name="ident")

        nc.gpsimd.memset(x_s[:].bitcast(I32), 0)
        with nc.allow_non_contiguous_dma(reason="one weight for each partition and row tile"):
            nc.scalar.dma_start(rob_sb[:], rob.rearrange("(t p) o -> p (t o)", p=P))
        make_identity(nc, ident[:])

        nc.sync.dma_start(field[0][:], grid_rows[0])
        inn_l = load_list("inn_l", inn)
        gh_l = load_list("gh_l", gh)
        nc.sync.dma_start(field[1][:], grid_rows[1])
        nc.sync.dma_start(x_w[:].bitcast(I32), x_words[0].rearrange("p n t -> p (n t)").bitcast(I32))
        offs_l = load_list("offs_l", offs)
        for q in range(P // QUADRANT):
            nc.sync.dma_start(
                x_s[QUADRANT * q : QUADRANT * q + 4, :].bitcast(I32),
                x_scales[0, 4 * q : 4 * q + 4, :].bitcast(I32),
            )
        nc.sync.dma_start(w1_raw[:], w1.rearrange("(p j) c -> p j c", j=PACK))
        nc.sync.dma_start(field[2][:], grid_rows[2])
        nc.sync.dma_start(field[3][:], grid_rows[3])
        c1_l = load_list("c1_l", c1)
        c2_l = load_list("c2_l", c2)
        c0_l = load_list("c0_l", c0)
        nc.sync.dma_start(w2_raw[:], w2.rearrange("(p j) c -> p j c", j=PACK))
        nc.sync.dma_start(unit_sb[:], unit.rearrange("h o -> (h o)").partition_broadcast(P))

        inner, ghost = {}, {}

        def look_up_grid(t):
            ghost[t] = keep.tile([P, S], F32, name="ghost%d" % t, tag="looked%d" % (2 * t), align_bytes=MX_ALIGN)
            inner[t] = keep.tile([P, S], F32, name="inner%d" % t, tag="looked%d" % (2 * t + 1), align_bytes=MX_ALIGN)
            weighted = keep.tile([P, U], F32, name="weighted%d" % t)
            nc.vector.tensor_scalar(weighted[:], field[t][:], rob_sb[:, t : t + 1], None, ALU.mult)
            nc.scalar.activation(ghost[t][:], weighted[:].indirect(gh_l[:]), ACT.Copy)
            if t == 0:
                nc.vector.tensor_copy(inner[t][:], weighted[:].indirect(inn_l[:]))
            else:
                nc.scalar.activation(inner[t][:], weighted[:].indirect(inn_l[:]), ACT.Copy)

        look_up_grid(0)
        look_up_grid(1)

        xg_w = keep.tile([P, S], U32, name="xg_w", align_bytes=MX_ALIGN)
        xg_s = keep.tile([P, S], U8, name="xg_s", align_bytes=MX_ALIGN)
        nc.vector.tensor_copy(xg_w[:], x_w[:].indirect(offs_l[:]))
        nc.vector.tensor_copy(xg_s[:], x_s[:].indirect(offs_l[:]))

        w1_bf = keep.tile([P, PACK * H], BF16, name="w1_bf", align_bytes=MX_ALIGN)
        w1_c = [
            keep.tile([P, P], U32, name="w1_c%d" % t, tag="looked%d" % (t + ROW_TILES), align_bytes=MX_ALIGN)
            for t in range(ROW_TILES)
        ]
        w1_s = keep.tile([P, H], U8, name="w1_s", align_bytes=MX_ALIGN)
        w1_dst = w1_bf[:].rearrange("p (t c i j) -> p t c j i", t=ROW_TILES, i=4, j=PACK)
        w1_src = w1_raw[:].rearrange("p j (t c i) -> p t c j i", t=ROW_TILES, i=4)
        for t in range(ROW_TILES):
            if t < W1_TILES_ON_VECTOR:
                nc.vector.tensor_copy(w1_dst[:, t], w1_src[:, t])
            else:
                nc.scalar.copy(w1_dst[:, t], w1_src[:, t])
        for t in range(ROW_TILES):
            nc.vector.quantize_mx(
                out=w1_c[t][:].bitcast(FP8X4),
                scales=w1_s[:, t * P : (t + 1) * P],
                in_=w1_bf[:, t * PACK * P : (t + 1) * PACK * P],
            )

        lap_t = [psum.tile([P, ROW_TILES, P], F32, name="lap_t%d" % b, tag="block%d" % b) for b in range(BLOCKS)]

        def add_up(t, terms, blocks):
            for term in range(TERMS):
                for b in blocks:
                    nc.tensor.matmul(
                        lap_t[b][:, t, :],
                        lhsT=terms[term][:, b * P : (b + 1) * P],
                        rhs=ident[:],
                        is_transpose=True,
                        start=(term == 0),
                        stop=(term == TERMS - 1),
                    )

        bounded = [keep.tile([P, S], F32, name="bounded%d" % t) for t in range(ROW_TILES)]
        part = [keep.tile([P, S], F32, name="part%d" % t) for t in range(ROW_TILES)]
        for t in range(ROW_TILES):
            y = psum.tile([P, S], F32, name="y", tag="work", bufs=2)
            nc.tensor.matmul_mx(
                out=y[:],
                lhsT=w1_c[t][:].bitcast(FP8X4),
                lhsT_scale=w1_s[:, t * P : (t + 1) * P],
                rhs=xg_w[:].bitcast(FP8X4),
                rhs_scale=xg_s[:],
                start=True,
                stop=True,
            )
            nc.scalar.activation(bounded[t][:], y[:], ACT.Tanh)
            if t % 2 == 1:
                look_up_grid(2 + t // 2)
        for t in range(ROW_TILES):
            nc.vector.scalar_tensor_tensor(part[t][:], bounded[t][:], 0.8, ghost[t][:], ALU.mult, ALU.subtract)
            nc.vector.tensor_tensor(field[t][:].indirect(gh_l[:]), part[t][:], inner[t][:], ALU.add)

        w2_bf = keep.tile([P, N, PACK], BF16, name="w2_bf", align_bytes=MX_ALIGN)
        w2_c = keep.tile([P, N], U32, name="w2_c", align_bytes=MX_ALIGN)
        w2_s = keep.tile([P, N], U8, name="w2_s", align_bytes=MX_ALIGN)
        nc.vector.tensor_copy(
            w2_bf[:].rearrange("p (c i) j -> p c j i", i=4),
            w2_raw[:].rearrange("p j (c i) -> p c j i", i=4),
        )
        nc.vector.quantize_mx(out=w2_c[:].bitcast(FP8X4), scales=w2_s[:], in_=w2_bf[:].rearrange("p c j -> p (c j)"))

        terms = [
            [keep.tile([P, W], F32, name="term%d_%d" % (term, t)) for term in range(TERMS)] for t in range(ROW_TILES)
        ]
        last = ROW_TILES - 1
        for t in range(last):
            nc.scalar.activation(terms[t][0][:], field[t][:].indirect(c1_l[:]), ACT.Copy)
            nc.scalar.activation(terms[t][1][:], field[t][:].indirect(c2_l[:]), ACT.Copy)
            nc.scalar.activation(terms[t][2][:], field[t][:].indirect(c0_l[:]), ACT.Copy, scale=-1.6)
            add_up(t, terms[t], range(BLOCKS))

        half_w, half_columns, half_blocks = W // 2, W // 2 // ENTRIES_PER_COLUMN, BLOCKS // 2
        for half in range(2):
            stencils = slice(half * half_w, (half + 1) * half_w)
            entries = slice(half * half_columns, (half + 1) * half_columns)
            nc.vector.tensor_copy(terms[last][0][:, stencils], field[last][:].indirect(c1_l[:, entries]))
            if half == 0:
                nc.vector.tensor_copy(terms[last][1][:, stencils], field[last][:].indirect(c2_l[:, entries]))
            else:
                nc.scalar.activation(terms[last][1][:, stencils], field[last][:].indirect(c2_l[:, entries]), ACT.Copy)
            nc.scalar.activation(
                terms[last][2][:, stencils], field[last][:].indirect(c0_l[:, entries]), ACT.Copy, scale=-1.6
            )
            add_up(last, terms[last], range(half * half_blocks, (half + 1) * half_blocks))

        out_v = out.rearrange("(h m) w -> m h w", m=P)
        for b in range(BLOCKS):
            hid_t = keep.tile([P, H], BF16, name="hid_t%d" % b)
            nc.vector.tensor_tensor(hid_t[:], lap_t[b][:].rearrange("w t p -> w (t p)"), unit_sb[:], ALU.mult)
            pairs = psum.tile([P, 2, P], F32, name="pairs", tag="work" if b < 2 else "spare", bufs=2)
            for u in range(2):
                nc.tensor.transpose(pairs[:, u, :], hid_t[:].bitcast(F32)[:, u::2], ident[:])
            hid = keep.tile([P, PACK * P], BF16, name="hid%d" % b, align_bytes=MX_ALIGN)
            nc.scalar.copy(
                hid[:].bitcast(F32).rearrange("p (w u) -> p w u", u=2), pairs[:].rearrange("p u w -> p w u")
            )
            hid_c = keep.tile([P, P], U32, name="hid_c%d" % b, align_bytes=MX_ALIGN)
            hid_s = keep.tile([P, P], U8, name="hid_s%d" % b, align_bytes=MX_ALIGN)
            nc.vector.quantize_mx(out=hid_c[:].bitcast(FP8X4), scales=hid_s[:], in_=hid[:])
            acc = psum.tile([P, N // P, P], F32, name="acc", tag="block%d" % b)
            for h in range(N // P):
                nc.tensor.matmul_mx(
                    out=acc[:, h, :],
                    lhsT=w2_c[:, h * P : (h + 1) * P].bitcast(FP8X4),
                    lhsT_scale=w2_s[:, h * P : (h + 1) * P],
                    rhs=hid_c[:].bitcast(FP8X4),
                    rhs_scale=hid_s[:],
                    start=True,
                    stop=True,
                )
            res = keep.tile([P, N // P, P], F32, name="res%d" % b)
            if b == BLOCKS - 2:
                nc.vector.tensor_copy(res[:], acc[:])
            else:
                nc.scalar.copy(res[:], acc[:])
            nc.sync.dma_start(out_v[:, :, b * P : (b + 1) * P], res[:])
